import numpy as np
import ml_dtypes


def mxq(x, axis, fmt="e4m3"):
    dtype, down = {"e4m3": (ml_dtypes.float8_e4m3fn, 7), "e5m2": (ml_dtypes.float8_e5m2, 14)}[fmt]
    v = np.moveaxis(np.asarray(x, np.float32).astype(ml_dtypes.bfloat16).astype(np.float64), axis, -1)
    blocks = v.reshape(v.shape[:-1] + (-1, 32))
    amax = np.abs(blocks).max(-1, keepdims=True)
    byte = np.maximum(np.where(amax > 0, np.frexp(amax)[1] - 1 + 127, 0) - down, 1)
    scale = np.exp2(byte - 127.0)
    codes = (blocks / scale).astype(np.float32).astype(dtype).astype(np.float64)
    return np.moveaxis((codes * scale).reshape(v.shape), -1, axis)


WIDE = False


def mx_kscale(k):
    if not WIDE:
        return np.ones(k)
    levels = np.array([10, -10, 5, -5, 0])
    if k % 512:
        return np.exp2(np.random.permutation(np.resize(levels, k // 32))).repeat(32)
    a = np.empty((k // 512, 16))
    for p in range(k // 512):
        a[p, :8] = np.random.permutation(np.resize(levels, 8))
        for g in range(8):
            far = levels[np.abs(levels - a[p, g]) >= 10]
            a[p, g + 8] = far[np.random.randint(len(far))]
    return np.exp2(a.ravel()).repeat(32)


def f64(x):
    return np.asarray(x).astype(np.float64)


def striped(idx):
    return np.tile(np.asarray(idx).reshape(-1, 16).T, (8, 1)).astype(np.uint16)


def unstriped(offs):
    return offs[:16].T.reshape(-1).astype(np.int64)


E2M1 = np.array([0.0, 0.5, 1.0, 1.5, 2.0, 3.0, 4.0, 6.0, -0.0, -0.5, -1.0, -1.5, -2.0, -3.0, -4.0, -6.0])


def pack_weight(w, fmt):
    k, n = w.shape
    w = f64(np.asarray(w, np.float32).astype(ml_dtypes.bfloat16)).reshape(k // 32, 32, n)
    amax = np.abs(w).max(1)
    if fmt == "e4m3":
        byte = np.frexp(amax)[1] - 1 + 127 - 7
    else:
        mant, ex = np.frexp(amax / 6.0)
        byte = np.where(mant > 0.5, ex, ex - 1) + 127
    byte = np.clip(np.where(amax > 0, byte, 1), 1, 254)
    scaled = (w * np.exp2(127.0 - byte)[:, None, :]).reshape(k, n).astype(np.float32)
    by_word = np.ascontiguousarray(scaled.reshape(k // 512, 128, 4, n).transpose(0, 1, 3, 2))
    if fmt == "e4m3":
        words = by_word.astype(ml_dtypes.float8_e4m3fn).view(np.uint8)
    else:
        c = by_word.astype(ml_dtypes.float4_e2m1fn).view(np.uint8) & 0xF
        words = (c[..., 0::2] | (c[..., 1::2] << 4)).reshape(k // 512, 128, 2 * n)
    return np.ascontiguousarray(words), np.ascontiguousarray(byte.astype(np.uint8).reshape(k // 512, 16, n))


def unpack_weight(words, scales, fmt):
    g, _, n = scales.shape
    words = np.ascontiguousarray(words).reshape(g, 128, n, -1)
    if fmt == "e4m3":
        vals = words.view(ml_dtypes.float8_e4m3fn).astype(np.float64)
    else:
        nib = np.empty((g, 128, n, 4), np.uint8)
        nib[..., 0::2] = words & 0xF
        nib[..., 1::2] = words >> 4
        vals = E2M1[nib]
    vals = vals * np.repeat(np.exp2(scales.astype(np.float64) - 127.0), 8, axis=1)[..., None]
    return vals.transpose(0, 1, 3, 2).reshape(g * 512, n)


def bf(x):
    return np.asarray(x, np.float32).astype(ml_dtypes.bfloat16)


def planes(Y):
    r, m = Y.shape
    b = f64(bf(Y)).reshape(r // 32, 32, m)
    amax = np.abs(b).max(1)
    byte = np.clip(np.where(amax > 0, np.frexp(amax)[1] - 1 + 127 - 7, 1), 1, 254)
    codes = (b * np.exp2(127.0 - byte)[:, None, :]).reshape(r, m).astype(np.float32).astype(ml_dtypes.float8_e4m3fn).view(np.uint8)
    words = codes.reshape(r // 512, 128, 4, m).transpose(0, 1, 3, 2)
    return np.ascontiguousarray(words), np.ascontiguousarray(byte.astype(np.uint8).reshape(r // 512, 16, m))


D, T, I, J, U, E, N = 512, 2048, 512, 512, 1024, 512, 64


def setup_inputs():
    n = np.random.standard_normal
    idx = np.random.permutation(T)[:I]
    idx2 = np.random.permutation(U)[:J]
    idx3 = np.random.permutation(U)[:J]
    idx4 = np.random.permutation(U)[:J]
    fd = mx_kscale(D)
    fi = mx_kscale(I)
    ti = np.ones(T)
    ti[idx] = fi
    keysp = pack_weight(n((D, T)) / fd[:, None], "e2m1")
    return {
        "keys_words": keysp[0],
        "keys_scales": keysp[1],
        "notes": (n((D, U)) * 1.0 / np.sqrt(D) * fd[:, None]).astype(np.float32),
        "rowf": (np.random.uniform(0.02, 0.08, (I, 1)) * fi[:, None]).astype(np.float32),
        "vals": (n((E, T)) / ti).astype(np.float32),
        "offs": striped(idx),
        "offs2": striped(idx2),
        "offs3": striped(idx3),
        "offs4": striped(idx4),
    }


def reference(keys_words, keys_scales, notes, rowf, vals, offs, offs2, offs3, offs4):
    idx = unstriped(offs)
    idx2 = unstriped(offs2)
    idx3 = unstriped(offs3)
    idx4 = unstriped(offs4)
    keysu = unpack_weight(keys_words, keys_scales, "e2m1")
    keysidxg = keysu[:, idx]
    notesq = mxq(f64(notes), 0, "e4m3")
    g1 = keysidxg.T @ notesq
    lo2 = np.minimum(g1[:, idx2], g1[:, idx3])
    hi2 = np.maximum(g1[:, idx2], g1[:, idx3])
    g0 = np.maximum(lo2, np.minimum(hi2, g1[:, idx4]))
    gr1 = g0 * f64(rowf)
    vt1 = f64(vals)[:, idx].T
    vt1q = mxq(vt1, 0, "e4m3")
    gr1q = mxq(gr1, 0, "e4m3")
    o = vt1q.T @ gr1q
    y = o.reshape(E, N, J // N).max(axis=2)
    words, scales = planes(y)
    return y, words, scales

@@ -1,0 +1,234 @@
+from contextlib import ExitStack
+
+import concourse.mybir as mybir
+from concourse.masks import make_identity
+
+F32 = mybir.dt.float32
+BF16 = mybir.dt.bfloat16
+I32 = mybir.dt.int32
+U32 = mybir.dt.uint32
+U16 = mybir.dt.uint16
+U8 = mybir.dt.uint8
+FP8X4 = mybir.dt.float8_e4m3fn_x4
+FP4X4 = mybir.dt.float4_e2m1fn_x4
+ALU = mybir.AluOpType
+COPY = mybir.ActivationFunctionType.Copy
+
+P = 128
+PACK = 4
+T, I, J, U, RUN = 2048, 512, 512, 1024, 8
+N = J // RUN
+PIECE = 256
+HALF = 512
+
+FLOPS = 2 * 512 * I * U + 2 * I * 512 * J
+
+
+def tile_attend_tab_middleof3_bestruns_pl_kernel(
+    tc, keys_words, keys_scales, notes, rowf, vals, offs, offs2, offs3, offs4, out_0, out_1, out_2
+):
+    nc = tc.nc
+    with ExitStack() as ctx:
+        sb = ctx.enter_context(tc.tile_pool(name="sb", bufs=1))
+        ring = ctx.enter_context(tc.tile_pool(name="ring", bufs=2))
+        psum = ctx.enter_context(tc.psum_pool(name="psum", bufs=8))
+
+        def new_tile(shape, dtype, name):
+            return sb.tile(shape, dtype, name=name, align_bytes=64)
+
+        def vector_tile(shape, dtype, name):
+            return sb.tile(shape, dtype, name=name, tag="vector_order", bufs=24, align_bytes=64)
+
+        def scalar_tile(shape, dtype, name):
+            return sb.tile(shape, dtype, name=name, tag="scalar_order", bufs=16, align_bytes=64)
+
+        list_i = new_tile([P, I // 16], U16, "list_i")
+        lists_j = [new_tile([P, J // 16], U16, "list_j%d" % k) for k in range(3)]
+        key_words = new_tile([P, T], U16, "key_words")
+        key_scales = new_tile([P, T], U8, "key_scales")
+        nc.gpsimd.memset(key_scales[:].bitcast(I32), 0)
+        nc.sync.dma_start(list_i[:], offs)
+        for lst, src in zip(lists_j, (offs2, offs3, offs4)):
+            nc.sync.dma_start(lst[:], src)
+        nc.sync.dma_start(key_words[:].bitcast(I32), keys_words[0].bitcast(I32))
+        for q in range(4):
+            nc.scalar.dma_start(
+                key_scales[32 * q : 32 * q + 4, :].bitcast(I32), keys_scales[0, 4 * q : 4 * q + 4, :].bitcast(I32)
+            )
+        notes_v = notes.rearrange("(p t) u -> p t u", t=PACK)
+        notes_raw = []
+        for k in range(U // PIECE):
+            raw = new_tile([P, PACK, PIECE], F32, "notes_raw%d" % k)
+            nc.sync.dma_start(raw[:], notes_v[:, :, k * PIECE : (k + 1) * PIECE])
+            notes_raw.append(raw)
+        vals_v = vals.rearrange("(p r) t -> p r t", r=PACK)
+        vals_raw = []
+        for r in range(PACK):
+            raw = new_tile([P, T], F32, "vals_raw%d" % r)
+            nc.sync.dma_start(raw[:], vals_v[:, r, :])
+            vals_raw.append(raw)
+        row_factor = new_tile([P, PACK], F32, "row_factor")
+        nc.sync.dma_start(row_factor[:], rowf.rearrange("(p r) o -> p (r o)", r=PACK))
+
+        ident = new_tile([P, P], F32, "ident")
+        make_identity(nc, ident[:])
+
+        note_codes, note_scales, grouped = {}, {}, {}
+
+        def round_notes(k, on_vector):
+            grouped[k] = (vector_tile if on_vector else scalar_tile)([P, PIECE * PACK], BF16, "notes_bf%d" % k)
+            dst = grouped[k][:].rearrange("p (c i t) -> p c t i", i=4, t=PACK)
+            src = notes_raw[k][:].rearrange("p t (c i) -> p c t i", i=4)
+            if on_vector:
+                nc.vector.tensor_copy(dst, src)
+            else:
+                nc.scalar.copy(dst, src)
+
+        def quantize_notes(k):
+            h = k // 2
+            if k % 2 == 0:
+                note_codes[h] = vector_tile([P, HALF], U32, "note_codes%d" % h)
+                note_scales[h] = new_tile([P, HALF], U8, "note_scales%d" % h)
+            cols = slice((k % 2) * PIECE, (k % 2 + 1) * PIECE)
+            nc.vector.quantize_mx(note_codes[h][:, cols].bitcast(FP8X4), note_scales[h][:, cols], grouped[k][:])
+
+        picked_words = vector_tile([P, I], U16, "picked_words")
+        nc.vector.tensor_copy(picked_words[:], key_words[:].indirect(list_i[:]))
+        dealt_words = vector_tile([P, PACK, P], U16, "dealt_words")
+        nc.vector.tensor_copy(dealt_words[:], picked_words[:].rearrange("p (s r) -> p r s", r=PACK))
+        for k in range(3):
+            round_notes(k, False)
+        quantize_notes(0)
+        dealt_scales = vector_tile([P, PACK, P], U8, "dealt_scales")
+        nc.vector.tensor_copy(dealt_scales[:].rearrange("p r s -> p s r"), key_scales[:].indirect(list_i[:]))
+        quantize_notes(1)
+
+        g1 = [new_tile([P, U], F32, "g1_%d" % r) for r in range(PACK)]
+
+        def product1(r, h, on_vector):
+            bank = psum.tile([P, HALF], F32, name="bank_g", tag="bank")
+            nc.tensor.matmul_mx(
+                bank[:],
+                lhsT=dealt_words[:, r, :].bitcast(FP4X4),
+                lhsT_scale=dealt_scales[:, r, :],
+                rhs=note_codes[h][:].bitcast(FP8X4),
+                rhs_scale=note_scales[h][:],
+                start=True,
+                stop=True,
+            )
+            dst = g1[r][:, h * HALF : (h + 1) * HALF]
+            if on_vector:
+                nc.vector.tensor_copy(dst, bank[:])
+            else:
+                nc.scalar.copy(dst, bank[:])
+
+        for r in range(PACK):
+            product1(r, 0, False)
+        round_notes(3, True)
+        quantize_notes(2)
+        quantize_notes(3)
+        for r in range(PACK):
+            product1(r, 1, r == 0)
+
+        def look_up(r, k, on_vector):
+            picked = (vector_tile if on_vector else scalar_tile)([P, J], F32, "picked%d_%d" % (r, k))
+            if on_vector:
+                nc.vector.tensor_copy(picked[:], g1[r][:].indirect(lists_j[k][:]))
+            else:
+                nc.scalar.activation(picked[:], g1[r][:].indirect(lists_j[k][:]), COPY)
+            return picked
+
+        g0 = sb.tile([P, PACK, J], F32, name="g0", tag="g0", align_bytes=64)
+        on_vector = {(0, 0), (0, 1), (3, 0)}
+        picked = {}
+        order = [(0, 0), (0, 1), (0, 2), (1, 0), (1, 1), (1, 2), (2, 0), (2, 1), (2, 2), (3, 1), (3, 2)]
+        for r, k in order:
+            picked[r, k] = look_up(r, k, (r, k) in on_vector)
+        for r in range(PACK):
+            hi = vector_tile([P, J], F32, "hi%d" % r)
+            lo = vector_tile([P, J], F32, "lo%d" % r)
+            cut = vector_tile([P, J], F32, "cut%d" % r)
+            nc.vector.tensor_tensor(hi[:], picked[r, 0][:], picked[r, 1][:], ALU.max)
+            nc.vector.tensor_tensor(lo[:], picked[r, 0][:], picked[r, 1][:], ALU.min)
+            nc.vector.tensor_tensor(cut[:], hi[:], picked[r, 2][:], ALU.min)
+            if r == 0:
+                picked[3, 0] = look_up(3, 0, True)
+            nc.vector.tensor_tensor(g0[:, r, :], lo[:], cut[:], ALU.max)
+
+        gr1 = new_tile([P, J * PACK], BF16, "gr1")
+        nc.vector.tensor_tensor(
+            gr1[:].rearrange("p (c i t) -> p c t i", i=4, t=PACK),
+            g0[:].rearrange("p t (c i) -> p c t i", i=4),
+            row_factor[:].unsqueeze(1).unsqueeze(3).to_broadcast([P, J // 4, PACK, 4]),
+            ALU.mult,
+        )
+        gr1_codes = new_tile([P, J], U32, "gr1_codes")
+        gr1_scales = new_tile([P, J], U8, "gr1_scales")
+        nc.vector.quantize_mx(gr1_codes[:].bitcast(FP8X4), gr1_scales[:], gr1[:])
+
+        y = new_tile([P, PACK, N], F32, "y")
+        vt_scales = sb.tile([P, PACK, P], U8, name="vt_scales", tag="g0", align_bytes=64)
+        picked_vals, vt1, vt_codes = {}, {}, {}
+
+        def pick_vals(r):
+            picked_vals[r] = scalar_tile([P, I], BF16, "picked_vals%d" % r)
+            nc.scalar.activation(picked_vals[r][:], vals_raw[r][:].indirect(list_i[:]), COPY)
+
+        def turn_vals(r):
+            pairs = picked_vals[r][:].bitcast(F32)
+            turned = psum.tile([P, 2, P], F32, name="turned", tag="bank")
+            for u in range(2):
+                nc.tensor.transpose(turned[:, u, :], pairs[:, u : I // 2 : 2], ident[:])
+            vt1[r] = new_tile([P, P * PACK], BF16, "vt1_%d" % r)
+            nc.scalar.copy(
+                vt1[r][:].bitcast(F32).rearrange("p (e u) -> p e u", u=2), turned[:].rearrange("p u e -> p e u")
+            )
+
+        def quantize_vals(r):
+            vt_codes[r] = ring.tile([P, P], U32, name="vt_codes", align_bytes=64)
+            nc.vector.quantize_mx(vt_codes[r][:].bitcast(FP8X4), vt_scales[:, r, :], vt1[r][:])
+
+        banks_o = {}
+
+        def product2(r):
+            banks_o[r] = psum.tile([P, J], F32, name="bank_o", tag="bank")
+            nc.tensor.matmul_mx(
+                banks_o[r][:],
+                lhsT=vt_codes[r][:].bitcast(FP8X4),
+                lhsT_scale=vt_scales[:, r, :],
+                rhs=gr1_codes[:].bitcast(FP8X4),
+                rhs_scale=gr1_scales[:],
+                start=True,
+                stop=True,
+            )
+
+        def best_of_runs(r):
+            nc.vector.tensor_reduce(
+                y[:, r, :], banks_o[r][:].rearrange("p (n k) -> p n k", k=RUN), mybir.AxisListType.X, ALU.max
+            )
+
+        for r in range(PACK):
+            pick_vals(r)
+            if r > 0:
+                turn_vals(r - 1)
+        for r in range(2):
+            quantize_vals(r)
+            product2(r)
+        turn_vals(3)
+        for r in range(2, PACK):
+            best_of_runs(r - 2)
+            quantize_vals(r)
+            product2(r)
+        for r in range(2, PACK):
+            best_of_runs(r)
+
+        nc.sync.dma_start(out_0.rearrange("(p r) n -> p r n", r=PACK), y[:])
+        y_bf = new_tile([P, N * PACK], BF16, "y_bf")
+        nc.vector.tensor_copy(y_bf[:].rearrange("p (n r) -> p n r", r=PACK), y[:].rearrange("p r n -> p n r"))
+        y_codes = new_tile([P, N], U32, "y_codes")
+        y_scales = new_tile([P, N], U8, "y_scales")
+        nc.vector.quantize_mx(y_codes[:].bitcast(FP8X4), y_scales[:], y_bf[:])
+        nc.sync.dma_start(out_1[0].rearrange("p c r -> p (c r)").bitcast(I32), y_codes[:].bitcast(I32))
+        for q in range(4):
+            queue = nc.sync if q % 2 else nc.scalar
+            queue.dma_start(out_2[0, 4 * q : 4 * q + 4, :].bitcast(I32), y_scales[32 * q : 32 * q + 4, :].bitcast(I32))

@@ -30,45 +30,51 @@ def tile_attend_tab_middleof3_bestruns_pl_kernel(
     nc = tc.nc
     with ExitStack() as ctx:
         sb = ctx.enter_context(tc.tile_pool(name="sb", bufs=1))
-        ring = ctx.enter_context(tc.tile_pool(name="ring", bufs=2))
+        ring = ctx.enter_context(tc.tile_pool(name="ring", bufs=3))
         psum = ctx.enter_context(tc.psum_pool(name="psum", bufs=8))
 
         def new_tile(shape, dtype, name):
             return sb.tile(shape, dtype, name=name, align_bytes=64)
 
         def vector_tile(shape, dtype, name):
-            return sb.tile(shape, dtype, name=name, tag="vector_order", bufs=24, align_bytes=64)
+            return sb.tile(shape, dtype, name=name, tag="vector_order", bufs=31, align_bytes=64)
 
         def scalar_tile(shape, dtype, name):
-            return sb.tile(shape, dtype, name=name, tag="scalar_order", bufs=16, align_bytes=64)
+            return sb.tile(shape, dtype, name=name, tag="scalar_order", bufs=14, align_bytes=64)
+
+        def load_tile(shape, dtype, name):
+            return sb.tile(shape, dtype, name=name, tag="load_order", bufs=12, align_bytes=64)
 
         list_i = new_tile([P, I // 16], U16, "list_i")
-        lists_j = [new_tile([P, J // 16], U16, "list_j%d" % k) for k in range(3)]
         key_words = new_tile([P, T], U16, "key_words")
         key_scales = new_tile([P, T], U8, "key_scales")
         nc.gpsimd.memset(key_scales[:].bitcast(I32), 0)
         nc.sync.dma_start(list_i[:], offs)
-        for lst, src in zip(lists_j, (offs2, offs3, offs4)):
-            nc.sync.dma_start(lst[:], src)
         nc.sync.dma_start(key_words[:].bitcast(I32), keys_words[0].bitcast(I32))
         for q in range(4):
-            nc.scalar.dma_start(
+            nc.sync.dma_start(
                 key_scales[32 * q : 32 * q + 4, :].bitcast(I32), keys_scales[0, 4 * q : 4 * q + 4, :].bitcast(I32)
             )
         notes_v = notes.rearrange("(p t) u -> p t u", t=PACK)
         notes_raw = []
         for k in range(U // PIECE):
-            raw = new_tile([P, PACK, PIECE], F32, "notes_raw%d" % k)
+            raw = load_tile([P, PACK, PIECE], F32, "notes_raw%d" % k)
             nc.sync.dma_start(raw[:], notes_v[:, :, k * PIECE : (k + 1) * PIECE])
             notes_raw.append(raw)
+        lists_j = []
+        for k, src in enumerate((offs2, offs3, offs4)):
+            lst = load_tile([P, J // 16], U16, "list_j%d" % k)
+            nc.sync.dma_start(lst[:], src)
+            lists_j.append(lst)
         vals_v = vals.rearrange("(p r) t -> p r t", r=PACK)
         vals_raw = []
         for r in range(PACK):
-            raw = new_tile([P, T], F32, "vals_raw%d" % r)
+            raw = load_tile([P, T], F32, "vals_raw%d" % r)
             nc.sync.dma_start(raw[:], vals_v[:, r, :])
             vals_raw.append(raw)
-        row_factor = new_tile([P, PACK], F32, "row_factor")
+        row_factor = load_tile([P, PACK], F32, "row_factor")
         nc.sync.dma_start(row_factor[:], rowf.rearrange("(p r) o -> p (r o)", r=PACK))
+
 
         ident = new_tile([P, P], F32, "ident")
         make_identity(nc, ident[:])
@@ -95,80 +101,88 @@ def tile_attend_tab_middleof3_bestruns_pl_kernel(
         picked_words = vector_tile([P, I], U16, "picked_words")
         nc.vector.tensor_copy(picked_words[:], key_words[:].indirect(list_i[:]))
         dealt_words = vector_tile([P, PACK, P], U16, "dealt_words")
-        nc.vector.tensor_copy(dealt_words[:], picked_words[:].rearrange("p (s r) -> p r s", r=PACK))
-        for k in range(3):
-            round_notes(k, False)
-        quantize_notes(0)
+        nc.vector.tensor_copy(
+            dealt_words[:].rearrange("p r (c s) -> p c r s", s=8),
+            picked_words[:].rearrange("p (c s r) -> p c r s", s=8, r=PACK),
+        )
+        round_notes(0, False)
         dealt_scales = vector_tile([P, PACK, P], U8, "dealt_scales")
         nc.vector.tensor_copy(dealt_scales[:].rearrange("p r s -> p s r"), key_scales[:].indirect(list_i[:]))
-        quantize_notes(1)
+        quantize_notes(0)
 
-        g1 = [new_tile([P, U], F32, "g1_%d" % r) for r in range(PACK)]
+        g1 = new_tile([P, PACK, U], F32, "g1")
 
-        def product1(r, h, on_vector):
-            bank = psum.tile([P, HALF], F32, name="bank_g", tag="bank")
-            nc.tensor.matmul_mx(
-                bank[:],
-                lhsT=dealt_words[:, r, :].bitcast(FP4X4),
-                lhsT_scale=dealt_scales[:, r, :],
-                rhs=note_codes[h][:].bitcast(FP8X4),
-                rhs_scale=note_scales[h][:],
-                start=True,
-                stop=True,
-            )
-            dst = g1[r][:, h * HALF : (h + 1) * HALF]
-            if on_vector:
-                nc.vector.tensor_copy(dst, bank[:])
-            else:
-                nc.scalar.copy(dst, bank[:])
+        def product1(k, engines):
+            h = k // 2
+            cols = slice((k % 2) * PIECE, (k % 2 + 1) * PIECE)
+            for a, on_vector in enumerate(engines):
+                bank = psum.tile([P, 2, PIECE], F32, name="bank_g", tag="bank")
+                for b in range(2):
+                    r = 2 * a + b
+                    nc.tensor.matmul_mx(
+                        bank[:, b, :],
+                        lhsT=dealt_words[:, r, :].bitcast(FP4X4),
+                        lhsT_scale=dealt_scales[:, r, :],
+                        rhs=note_codes[h][:, cols].bitcast(FP8X4),
+                        rhs_scale=note_scales[h][:, cols],
+                        start=True,
+                        stop=True,
+                    )
+                dst = g1[:, 2 * a : 2 * a + 2, k * PIECE : (k + 1) * PIECE]
+                if on_vector:
+                    nc.vector.tensor_copy(dst, bank[:])
+                else:
+                    nc.scalar.copy(dst, bank[:])
 
-        for r in range(PACK):
-            product1(r, 0, False)
-        round_notes(3, True)
-        quantize_notes(2)
-        quantize_notes(3)
-        for r in range(PACK):
-            product1(r, 1, r == 0)
+        product1(0, (False, False))
+        for k in range(1, U // PIECE):
+            round_notes(k, True)
+            quantize_notes(k)
+            product1(k, (k == 3, False))
 
-        def look_up(r, k, on_vector):
-            picked = (vector_tile if on_vector else scalar_tile)([P, J], F32, "picked%d_%d" % (r, k))
-            if on_vector:
-                nc.vector.tensor_copy(picked[:], g1[r][:].indirect(lists_j[k][:]))
-            else:
-                nc.scalar.activation(picked[:], g1[r][:].indirect(lists_j[k][:]), COPY)
-            return picked
-
-        g0 = sb.tile([P, PACK, J], F32, name="g0", tag="g0", align_bytes=64)
-        on_vector = {(0, 0), (0, 1), (3, 0)}
         picked = {}
-        order = [(0, 0), (0, 1), (0, 2), (1, 0), (1, 1), (1, 2), (2, 0), (2, 1), (2, 2), (3, 1), (3, 2)]
-        for r, k in order:
-            picked[r, k] = look_up(r, k, (r, k) in on_vector)
-        for r in range(PACK):
-            hi = vector_tile([P, J], F32, "hi%d" % r)
-            lo = vector_tile([P, J], F32, "lo%d" % r)
-            cut = vector_tile([P, J], F32, "cut%d" % r)
-            nc.vector.tensor_tensor(hi[:], picked[r, 0][:], picked[r, 1][:], ALU.max)
-            nc.vector.tensor_tensor(lo[:], picked[r, 0][:], picked[r, 1][:], ALU.min)
-            nc.vector.tensor_tensor(cut[:], hi[:], picked[r, 2][:], ALU.min)
-            if r == 0:
-                picked[3, 0] = look_up(3, 0, True)
-            nc.vector.tensor_tensor(g0[:, r, :], lo[:], cut[:], ALU.max)
 
-        gr1 = new_tile([P, J * PACK], BF16, "gr1")
-        nc.vector.tensor_tensor(
-            gr1[:].rearrange("p (c i t) -> p c t i", i=4, t=PACK),
-            g0[:].rearrange("p t (c i) -> p c t i", i=4),
-            row_factor[:].unsqueeze(1).unsqueeze(3).to_broadcast([P, J // 4, PACK, 4]),
-            ALU.mult,
-        )
-        gr1_codes = new_tile([P, J], U32, "gr1_codes")
-        gr1_scales = new_tile([P, J], U8, "gr1_scales")
-        nc.vector.quantize_mx(gr1_codes[:].bitcast(FP8X4), gr1_scales[:], gr1[:])
+        def look_up(r, k, on_vector, part=slice(0, J)):
+            if (r, k) not in picked:
+                picked[r, k] = (vector_tile if on_vector else scalar_tile)([P, J], F32, "picked%d_%d" % (r, k))
+            window = g1[:, r, :].indirect(lists_j[k][:, part.start // 16 : part.stop // 16])
+            if on_vector:
+                nc.vector.tensor_copy(picked[r, k][:, part], window)
+            else:
+                nc.scalar.activation(picked[r, k][:, part], window, COPY)
+
+        g0 = new_tile([P, PACK, J], F32, "g0")
+        hi, lo, cut = {}, {}, {}
+
+        def bounds(r):
+            hi[r] = vector_tile([P, J], F32, "hi%d" % r)
+            lo[r] = vector_tile([P, J], F32, "lo%d" % r)
+            nc.vector.tensor_tensor(hi[r][:], picked[r, 0][:], picked[r, 1][:], ALU.max)
+            nc.vector.tensor_tensor(lo[r][:], picked[r, 0][:], picked[r, 1][:], ALU.min)
+
+        def middle(r, between):
+            cut[r] = vector_tile([P, J], F32, "cut%d" % r)
+            nc.vector.tensor_tensor(cut[r][:], hi[r][:], picked[r, 2][:], ALU.min)
+            between()
+            nc.vector.tensor_tensor(g0[:, r, :], lo[r][:], cut[r][:], ALU.max)
+
+        look_up(0, 0, True)
+        look_up(0, 1, True)
+        for r, k in ((0, 2), (1, 0), (1, 1), (1, 2), (2, 0), (2, 1), (2, 2)):
+            look_up(r, k, False)
+        bounds(0)
+        middle(0, lambda: look_up(3, 0, True))
+        bounds(1)
+        middle(1, lambda: None)
+        look_up(3, 1, False)
+        look_up(3, 2, False)
+        for r in (2, 3):
+            bounds(r)
+            middle(r, lambda: None)
 
         y = new_tile([P, PACK, N], F32, "y")
-        vt_scales = sb.tile([P, PACK, P], U8, name="vt_scales", tag="g0", align_bytes=64)
-        picked_vals, vt1, vt_codes = {}, {}, {}
+        picked_vals, vt1, vt_codes, vt_scales, gr1, gr1_codes, gr1_scales, banks_o = {}, {}, {}, {}, {}, {}, {}, {}
+        JH = J // 2
 
         def pick_vals(r):
             picked_vals[r] = scalar_tile([P, I], BF16, "picked_vals%d" % r)
@@ -186,21 +200,35 @@ def tile_attend_tab_middleof3_bestruns_pl_kernel(
 
         def quantize_vals(r):
             vt_codes[r] = ring.tile([P, P], U32, name="vt_codes", align_bytes=64)
-            nc.vector.quantize_mx(vt_codes[r][:].bitcast(FP8X4), vt_scales[:, r, :], vt1[r][:])
+            vt_scales[r] = vector_tile([P, P], U8, "vt_scales%d" % r)
+            nc.vector.quantize_mx(vt_codes[r][:].bitcast(FP8X4), vt_scales[r][:], vt1[r][:])
 
-        banks_o = {}
+        def scale_rows(h):
+            gr1[h] = vector_tile([P, JH * PACK], BF16, "gr1_%d" % h)
+            nc.vector.tensor_tensor(
+                gr1[h][:].rearrange("p (c i t) -> p c t i", i=4, t=PACK),
+                g0[:, :, h * JH : (h + 1) * JH].rearrange("p t (c i) -> p c t i", i=4),
+                row_factor[:].unsqueeze(1).unsqueeze(3).to_broadcast([P, JH // 4, PACK, 4]),
+                ALU.mult,
+            )
+
+        def quantize_table(h):
+            gr1_codes[h] = vector_tile([P, JH], U32, "gr1_codes%d" % h)
+            gr1_scales[h] = new_tile([P, JH], U8, "gr1_scales%d" % h)
+            nc.vector.quantize_mx(gr1_codes[h][:].bitcast(FP8X4), gr1_scales[h][:], gr1[h][:])
 
         def product2(r):
             banks_o[r] = psum.tile([P, J], F32, name="bank_o", tag="bank")
-            nc.tensor.matmul_mx(
-                banks_o[r][:],
-                lhsT=vt_codes[r][:].bitcast(FP8X4),
-                lhsT_scale=vt_scales[:, r, :],
-                rhs=gr1_codes[:].bitcast(FP8X4),
-                rhs_scale=gr1_scales[:],
-                start=True,
-                stop=True,
-            )
+            for h in range(2):
+                nc.tensor.matmul_mx(
+                    banks_o[r][:, h * JH : (h + 1) * JH],
+                    lhsT=vt_codes[r][:].bitcast(FP8X4),
+                    lhsT_scale=vt_scales[r][:],
+                    rhs=gr1_codes[h][:].bitcast(FP8X4),
+                    rhs_scale=gr1_scales[h][:],
+                    start=True,
+                    stop=True,
+                )
 
         def best_of_runs(r):
             nc.vector.tensor_reduce(
@@ -211,16 +239,23 @@ def tile_attend_tab_middleof3_bestruns_pl_kernel(
             pick_vals(r)
             if r > 0:
                 turn_vals(r - 1)
-        for r in range(2):
-            quantize_vals(r)
-            product2(r)
+        scale_rows(0)
+        scale_rows(1)
+        quantize_table(0)
+        quantize_vals(0)
+        quantize_table(1)
+        quantize_vals(1)
+        product2(0)
+        product2(1)
         turn_vals(3)
-        for r in range(2, PACK):
-            best_of_runs(r - 2)
-            quantize_vals(r)
-            product2(r)
-        for r in range(2, PACK):
-            best_of_runs(r)
+        quantize_vals(2)
+        product2(2)
+        best_of_runs(0)
+        best_of_runs(1)
+        quantize_vals(3)
+        product2(3)
+        best_of_runs(2)
+        best_of_runs(3)
 
         nc.sync.dma_start(out_0.rearrange("(p r) n -> p r n", r=PACK), y[:])
         y_bf = new_tile([P, N * PACK], BF16, "y_bf")

@@ -37,7 +37,7 @@ def tile_attend_tab_middleof3_bestruns_pl_kernel(
             return sb.tile(shape, dtype, name=name, align_bytes=64)
 
         def vector_tile(shape, dtype, name):
-            return sb.tile(shape, dtype, name=name, tag="vector_order", bufs=31, align_bytes=64)
+            return sb.tile(shape, dtype, name=name, tag="vector_order", bufs=28, align_bytes=64)
 
         def scalar_tile(shape, dtype, name):
             return sb.tile(shape, dtype, name=name, tag="scalar_order", bufs=14, align_bytes=64)
@@ -100,14 +100,14 @@ def tile_attend_tab_middleof3_bestruns_pl_kernel(
 
         picked_words = vector_tile([P, I], U16, "picked_words")
         nc.vector.tensor_copy(picked_words[:], key_words[:].indirect(list_i[:]))
+        round_notes(0, False)
+        dealt_scales = vector_tile([P, PACK, P], U8, "dealt_scales")
+        nc.vector.tensor_copy(dealt_scales[:].rearrange("p r s -> p s r"), key_scales[:].indirect(list_i[:]))
         dealt_words = vector_tile([P, PACK, P], U16, "dealt_words")
         nc.vector.tensor_copy(
             dealt_words[:].rearrange("p r (c s) -> p c r s", s=8),
             picked_words[:].rearrange("p (c s r) -> p c r s", s=8, r=PACK),
         )
-        round_notes(0, False)
-        dealt_scales = vector_tile([P, PACK, P], U8, "dealt_scales")
-        nc.vector.tensor_copy(dealt_scales[:].rearrange("p r s -> p s r"), key_scales[:].indirect(list_i[:]))
         quantize_notes(0)
 
         g1 = new_tile([P, PACK, U], F32, "g1")
@@ -151,38 +151,60 @@ def tile_attend_tab_middleof3_bestruns_pl_kernel(
             else:
                 nc.scalar.activation(picked[r, k][:, part], window, COPY)
 
-        g0 = new_tile([P, PACK, J], F32, "g0")
-        hi, lo, cut = {}, {}, {}
+        JH = J // 2
+        halves = [slice(0, JH), slice(JH, J)]
+        scaled = new_tile([P, 2, PACK, JH], BF16, "scaled")
+        hi, lo, cut, g0 = {}, {}, {}, {}
 
-        def bounds(r):
-            hi[r] = vector_tile([P, J], F32, "hi%d" % r)
-            lo[r] = vector_tile([P, J], F32, "lo%d" % r)
-            nc.vector.tensor_tensor(hi[r][:], picked[r, 0][:], picked[r, 1][:], ALU.max)
-            nc.vector.tensor_tensor(lo[r][:], picked[r, 0][:], picked[r, 1][:], ALU.min)
+        def pair(op, name, in0, in1):
+            out = vector_tile(list(in0.shape), F32, name)
+            nc.vector.tensor_tensor(out[:], in0, in1, op)
+            return out
 
-        def middle(r, between):
-            cut[r] = vector_tile([P, J], F32, "cut%d" % r)
-            nc.vector.tensor_tensor(cut[r][:], hi[r][:], picked[r, 2][:], ALU.min)
-            between()
-            nc.vector.tensor_tensor(g0[:, r, :], lo[r][:], cut[r][:], ALU.max)
+        def upper(r):
+            hi[r] = pair(ALU.max, "hi%d" % r, picked[r, 0][:], picked[r, 1][:])
+
+        def lower(r):
+            lo[r] = pair(ALU.min, "lo%d" % r, picked[r, 0][:], picked[r, 1][:])
+
+        def capped(r):
+            cut[r] = pair(ALU.min, "cut%d" % r, hi[r][:], picked[r, 2][:])
+
+        def middle(r):
+            g0[r] = pair(ALU.max, "g0_%d" % r, lo[r][:], cut[r][:])
+
+        def scale_rows(r):
+            nc.vector.tensor_scalar_mul(
+                scaled[:, :, r, :], g0[r][:].rearrange("p (h j) -> p h j", h=2), row_factor[:, r : r + 1]
+            )
 
         look_up(0, 0, True)
         look_up(0, 1, True)
         for r, k in ((0, 2), (1, 0), (1, 1), (1, 2), (2, 0), (2, 1), (2, 2)):
             look_up(r, k, False)
-        bounds(0)
-        middle(0, lambda: look_up(3, 0, True))
-        bounds(1)
-        middle(1, lambda: None)
-        look_up(3, 1, False)
+        look_up(3, 1, False, halves[1])
         look_up(3, 2, False)
-        for r in (2, 3):
-            bounds(r)
-            middle(r, lambda: None)
+        look_up(3, 0, True)
+        upper(0)
+        lower(0)
+        capped(0)
+        for r in range(PACK - 1):
+            upper(r + 1)
+            middle(r)
+            lower(r + 1)
+            scale_rows(r)
+            if r + 1 < PACK - 1:
+                capped(r + 1)
+            if r == 0:
+                look_up(3, 1, True, halves[0])
+        last = PACK - 1
+        cuts = [pair(ALU.min, "cut_last%d" % h, hi[last][:, halves[h]], picked[last, 2][:, halves[h]]) for h in range(2)]
+        mids = [pair(ALU.max, "g0_last%d" % h, lo[last][:, halves[h]], cuts[h][:]) for h in range(2)]
+        for h in range(2):
+            nc.vector.tensor_scalar_mul(scaled[:, h, last, :], mids[h][:], row_factor[:, last : last + 1])
 
         y = new_tile([P, PACK, N], F32, "y")
         picked_vals, vt1, vt_codes, vt_scales, gr1, gr1_codes, gr1_scales, banks_o = {}, {}, {}, {}, {}, {}, {}, {}
-        JH = J // 2
 
         def pick_vals(r):
             picked_vals[r] = scalar_tile([P, I], BF16, "picked_vals%d" % r)
@@ -203,13 +225,11 @@ def tile_attend_tab_middleof3_bestruns_pl_kernel(
             vt_scales[r] = vector_tile([P, P], U8, "vt_scales%d" % r)
             nc.vector.quantize_mx(vt_codes[r][:].bitcast(FP8X4), vt_scales[r][:], vt1[r][:])
 
-        def scale_rows(h):
+        def weave(h):
             gr1[h] = vector_tile([P, JH * PACK], BF16, "gr1_%d" % h)
-            nc.vector.tensor_tensor(
+            nc.vector.tensor_copy(
                 gr1[h][:].rearrange("p (c i t) -> p c t i", i=4, t=PACK),
-                g0[:, :, h * JH : (h + 1) * JH].rearrange("p t (c i) -> p c t i", i=4),
-                row_factor[:].unsqueeze(1).unsqueeze(3).to_broadcast([P, JH // 4, PACK, 4]),
-                ALU.mult,
+                scaled[:, h].rearrange("p t (c i) -> p c t i", i=4),
             )
 
         def quantize_table(h):
@@ -239,8 +259,8 @@ def tile_attend_tab_middleof3_bestruns_pl_kernel(
             pick_vals(r)
             if r > 0:
                 turn_vals(r - 1)
-        scale_rows(0)
-        scale_rows(1)
+        weave(0)
+        weave(1)
         quantize_table(0)
         quantize_vals(0)
         quantize_table(1)

from contextlib import ExitStack

import concourse.mybir as mybir
from concourse.masks import make_identity

F32 = mybir.dt.float32
BF16 = mybir.dt.bfloat16
I32 = mybir.dt.int32
U32 = mybir.dt.uint32
U16 = mybir.dt.uint16
U8 = mybir.dt.uint8
FP8X4 = mybir.dt.float8_e4m3fn_x4
FP4X4 = mybir.dt.float4_e2m1fn_x4
ALU = mybir.AluOpType
COPY = mybir.ActivationFunctionType.Copy

P = 128
PACK = 4
T, I, J, U, RUN = 2048, 512, 512, 1024, 8
N = J // RUN
PIECE = 256
HALF = 512

FLOPS = 2 * 512 * I * U + 2 * I * 512 * J


def tile_attend_tab_middleof3_bestruns_pl_kernel(
    tc, keys_words, keys_scales, notes, rowf, vals, offs, offs2, offs3, offs4, out_0, out_1, out_2
):
    nc = tc.nc
    with ExitStack() as ctx:
        sb = ctx.enter_context(tc.tile_pool(name="sb", bufs=1))
        ring = ctx.enter_context(tc.tile_pool(name="ring", bufs=3))
        psum = ctx.enter_context(tc.psum_pool(name="psum", bufs=8))

        def new_tile(shape, dtype, name):
            return sb.tile(shape, dtype, name=name, align_bytes=64)

        def vector_tile(shape, dtype, name):
            return sb.tile(shape, dtype, name=name, tag="vector_order", bufs=28, align_bytes=64)

        def scalar_tile(shape, dtype, name):
            return sb.tile(shape, dtype, name=name, tag="scalar_order", bufs=14, align_bytes=64)

        def load_tile(shape, dtype, name):
            return sb.tile(shape, dtype, name=name, tag="load_order", bufs=12, align_bytes=64)

        list_i = new_tile([P, I // 16], U16, "list_i")
        key_words = new_tile([P, T], U16, "key_words")
        key_scales = new_tile([P, T], U8, "key_scales")
        nc.gpsimd.memset(key_scales[:].bitcast(I32), 0)
        nc.sync.dma_start(list_i[:], offs)
        nc.sync.dma_start(key_words[:].bitcast(I32), keys_words[0].bitcast(I32))
        for q in range(4):
            nc.sync.dma_start(
                key_scales[32 * q : 32 * q + 4, :].bitcast(I32), keys_scales[0, 4 * q : 4 * q + 4, :].bitcast(I32)
            )
        notes_v = notes.rearrange("(p t) u -> p t u", t=PACK)
        notes_raw = []
        for k in range(U // PIECE):
            raw = load_tile([P, PACK, PIECE], F32, "notes_raw%d" % k)
            nc.sync.dma_start(raw[:], notes_v[:, :, k * PIECE : (k + 1) * PIECE])
            notes_raw.append(raw)
        lists_j = []
        for k, src in enumerate((offs2, offs3, offs4)):
            lst = load_tile([P, J // 16], U16, "list_j%d" % k)
            nc.sync.dma_start(lst[:], src)
            lists_j.append(lst)
        vals_v = vals.rearrange("(p r) t -> p r t", r=PACK)
        vals_raw = []
        for r in range(PACK):
            raw = load_tile([P, T], F32, "vals_raw%d" % r)
            nc.sync.dma_start(raw[:], vals_v[:, r, :])
            vals_raw.append(raw)
        row_factor = load_tile([P, PACK], F32, "row_factor")
        nc.sync.dma_start(row_factor[:], rowf.rearrange("(p r) o -> p (r o)", r=PACK))


        ident = new_tile([P, P], F32, "ident")
        make_identity(nc, ident[:])

        note_codes, note_scales, grouped = {}, {}, {}

        def round_notes(k, on_vector):
            grouped[k] = (vector_tile if on_vector else scalar_tile)([P, PIECE * PACK], BF16, "notes_bf%d" % k)
            dst = grouped[k][:].rearrange("p (c i t) -> p c t i", i=4, t=PACK)
            src = notes_raw[k][:].rearrange("p t (c i) -> p c t i", i=4)
            if on_vector:
                nc.vector.tensor_copy(dst, src)
            else:
                nc.scalar.copy(dst, src)

        def quantize_notes(k):
            h = k // 2
            if k % 2 == 0:
                note_codes[h] = vector_tile([P, HALF], U32, "note_codes%d" % h)
                note_scales[h] = new_tile([P, HALF], U8, "note_scales%d" % h)
            cols = slice((k % 2) * PIECE, (k % 2 + 1) * PIECE)
            nc.vector.quantize_mx(note_codes[h][:, cols].bitcast(FP8X4), note_scales[h][:, cols], grouped[k][:])

        picked_words = vector_tile([P, I], U16, "picked_words")
        nc.vector.tensor_copy(picked_words[:], key_words[:].indirect(list_i[:]))
        round_notes(0, False)
        dealt_scales = vector_tile([P, PACK, P], U8, "dealt_scales")
        nc.vector.tensor_copy(dealt_scales[:].rearrange("p r s -> p s r"), key_scales[:].indirect(list_i[:]))
        dealt_words = vector_tile([P, PACK, P], U16, "dealt_words")
        nc.vector.tensor_copy(
            dealt_words[:].rearrange("p r (c s) -> p c r s", s=8),
            picked_words[:].rearrange("p (c s r) -> p c r s", s=8, r=PACK),
        )
        quantize_notes(0)

        g1 = new_tile([P, PACK, U], F32, "g1")

        def product1(k, engines):
            h = k // 2
            cols = slice((k % 2) * PIECE, (k % 2 + 1) * PIECE)
            for a, on_vector in enumerate(engines):
                bank = psum.tile([P, 2, PIECE], F32, name="bank_g", tag="bank")
                for b in range(2):
                    r = 2 * a + b
                    nc.tensor.matmul_mx(
                        bank[:, b, :],
                        lhsT=dealt_words[:, r, :].bitcast(FP4X4),
                        lhsT_scale=dealt_scales[:, r, :],
                        rhs=note_codes[h][:, cols].bitcast(FP8X4),
                        rhs_scale=note_scales[h][:, cols],
                        start=True,
                        stop=True,
                    )
                dst = g1[:, 2 * a : 2 * a + 2, k * PIECE : (k + 1) * PIECE]
                if on_vector:
                    nc.vector.tensor_copy(dst, bank[:])
                else:
                    nc.scalar.copy(dst, bank[:])

        product1(0, (False, False))
        for k in range(1, U // PIECE):
            round_notes(k, True)
            quantize_notes(k)
            product1(k, (k == 3, False))

        picked = {}

        def look_up(r, k, on_vector, part=slice(0, J)):
            if (r, k) not in picked:
                picked[r, k] = (vector_tile if on_vector else scalar_tile)([P, J], F32, "picked%d_%d" % (r, k))
            window = g1[:, r, :].indirect(lists_j[k][:, part.start // 16 : part.stop // 16])
            if on_vector:
                nc.vector.tensor_copy(picked[r, k][:, part], window)
            else:
                nc.scalar.activation(picked[r, k][:, part], window, COPY)

        JH = J // 2
        halves = [slice(0, JH), slice(JH, J)]
        scaled = new_tile([P, 2, PACK, JH], BF16, "scaled")
        hi, lo, cut, g0 = {}, {}, {}, {}

        def pair(op, name, in0, in1):
            out = vector_tile(list(in0.shape), F32, name)
            nc.vector.tensor_tensor(out[:], in0, in1, op)
            return out

        def upper(r):
            hi[r] = pair(ALU.max, "hi%d" % r, picked[r, 0][:], picked[r, 1][:])

        def lower(r):
            lo[r] = pair(ALU.min, "lo%d" % r, picked[r, 0][:], picked[r, 1][:])

        def capped(r):
            cut[r] = pair(ALU.min, "cut%d" % r, hi[r][:], picked[r, 2][:])

        def middle(r):
            g0[r] = pair(ALU.max, "g0_%d" % r, lo[r][:], cut[r][:])

        def scale_rows(r):
            nc.vector.tensor_scalar_mul(
                scaled[:, :, r, :], g0[r][:].rearrange("p (h j) -> p h j", h=2), row_factor[:, r : r + 1]
            )

        look_up(0, 0, True)
        look_up(0, 1, True)
        for r, k in ((0, 2), (1, 0), (1, 1), (1, 2), (2, 0), (2, 1), (2, 2)):
            look_up(r, k, False)
        look_up(3, 1, False, halves[1])
        look_up(3, 2, False)
        look_up(3, 0, True)
        upper(0)
        lower(0)
        capped(0)
        for r in range(PACK - 1):
            upper(r + 1)
            middle(r)
            lower(r + 1)
            scale_rows(r)
            if r + 1 < PACK - 1:
                capped(r + 1)
            if r == 0:
                look_up(3, 1, True, halves[0])
        last = PACK - 1
        cuts = [pair(ALU.min, "cut_last%d" % h, hi[last][:, halves[h]], picked[last, 2][:, halves[h]]) for h in range(2)]
        mids = [pair(ALU.max, "g0_last%d" % h, lo[last][:, halves[h]], cuts[h][:]) for h in range(2)]
        for h in range(2):
            nc.vector.tensor_scalar_mul(scaled[:, h, last, :], mids[h][:], row_factor[:, last : last + 1])

        y = new_tile([P, PACK, N], F32, "y")
        picked_vals, vt1, vt_codes, vt_scales, gr1, gr1_codes, gr1_scales, banks_o = {}, {}, {}, {}, {}, {}, {}, {}

        def pick_vals(r):
            picked_vals[r] = scalar_tile([P, I], BF16, "picked_vals%d" % r)
            nc.scalar.activation(picked_vals[r][:], vals_raw[r][:].indirect(list_i[:]), COPY)

        def turn_vals(r):
            pairs = picked_vals[r][:].bitcast(F32)
            turned = psum.tile([P, 2, P], F32, name="turned", tag="bank")
            for u in range(2):
                nc.tensor.transpose(turned[:, u, :], pairs[:, u : I // 2 : 2], ident[:])
            vt1[r] = new_tile([P, P * PACK], BF16, "vt1_%d" % r)
            nc.scalar.copy(
                vt1[r][:].bitcast(F32).rearrange("p (e u) -> p e u", u=2), turned[:].rearrange("p u e -> p e u")
            )

        def quantize_vals(r):
            vt_codes[r] = ring.tile([P, P], U32, name="vt_codes", align_bytes=64)
            vt_scales[r] = vector_tile([P, P], U8, "vt_scales%d" % r)
            nc.vector.quantize_mx(vt_codes[r][:].bitcast(FP8X4), vt_scales[r][:], vt1[r][:])

        def weave(h):
            gr1[h] = vector_tile([P, JH * PACK], BF16, "gr1_%d" % h)
            nc.vector.tensor_copy(
                gr1[h][:].rearrange("p (c i t) -> p c t i", i=4, t=PACK),
                scaled[:, h].rearrange("p t (c i) -> p c t i", i=4),
            )

        def quantize_table(h):
            gr1_codes[h] = vector_tile([P, JH], U32, "gr1_codes%d" % h)
            gr1_scales[h] = new_tile([P, JH], U8, "gr1_scales%d" % h)
            nc.vector.quantize_mx(gr1_codes[h][:].bitcast(FP8X4), gr1_scales[h][:], gr1[h][:])

        def product2(r):
            banks_o[r] = psum.tile([P, J], F32, name="bank_o", tag="bank")
            for h in range(2):
                nc.tensor.matmul_mx(
                    banks_o[r][:, h * JH : (h + 1) * JH],
                    lhsT=vt_codes[r][:].bitcast(FP8X4),
                    lhsT_scale=vt_scales[r][:],
                    rhs=gr1_codes[h][:].bitcast(FP8X4),
                    rhs_scale=gr1_scales[h][:],
                    start=True,
                    stop=True,
                )

        def best_of_runs(r):
            nc.vector.tensor_reduce(
                y[:, r, :], banks_o[r][:].rearrange("p (n k) -> p n k", k=RUN), mybir.AxisListType.X, ALU.max
            )

        for r in range(PACK):
            pick_vals(r)
            if r > 0:
                turn_vals(r - 1)
        weave(0)
        weave(1)
        quantize_table(0)
        quantize_vals(0)
        quantize_table(1)
        quantize_vals(1)
        product2(0)
        product2(1)
        turn_vals(3)
        quantize_vals(2)
        product2(2)
        best_of_runs(0)
        best_of_runs(1)
        quantize_vals(3)
        product2(3)
        best_of_runs(2)
        best_of_runs(3)

        nc.sync.dma_start(out_0.rearrange("(p r) n -> p r n", r=PACK), y[:])
        y_bf = new_tile([P, N * PACK], BF16, "y_bf")
        nc.vector.tensor_copy(y_bf[:].rearrange("p (n r) -> p n r", r=PACK), y[:].rearrange("p r n -> p n r"))
        y_codes = new_tile([P, N], U32, "y_codes")
        y_scales = new_tile([P, N], U8, "y_scales")
        nc.vector.quantize_mx(y_codes[:].bitcast(FP8X4), y_scales[:], y_bf[:])
        nc.sync.dma_start(out_1[0].rearrange("p c r -> p (c r)").bitcast(I32), y_codes[:].bitcast(I32))
        for q in range(4):
            queue = nc.sync if q % 2 else nc.scalar
            queue.dma_start(out_2[0, 4 * q : 4 * q + 4, :].bitcast(I32), y_scales[32 * q : 32 * q + 4, :].bitcast(I32))
